import numpy as np, ml_dtypes
CORES = [73,201,329,457,330]
N = 5
TOK, CAP, FF = 1024, 256, 1
def entries(a): return a.T.reshape(-1)
def pack(v, P): return np.ascontiguousarray(np.asarray(v, np.int32).reshape(-1, P).T)
def lists(rng, how):
    E = rng.integers(0, N, (N, TOK))
    if how == "hot": E[:] = rng.integers(N)
    if how == "none": E = (int(rng.integers(N)) + 1 + rng.integers(0, N - 1, (N, TOK))) % N
    if how == "skew": E = np.where(rng.random((N, TOK)) < 0.7, rng.integers(0, N, (N, 1)), E)
    if how == "even": E = np.stack([rng.permutation(np.arange(TOK) % N) for r in range(N)])
    if how == "own": E = np.repeat(np.arange(N).reshape(N, 1), TOK, axis=1)
    return {"ex": np.stack([pack(E[r], 16) for r in range(N)]), "pos": np.stack([pack(p, 16) for p in np.stack([np.array([np.sum(E[r, :t] == E[r, t]) for t in range(TOK)]) for r in range(N)])])}
def setup_inputs(rng):
    return dict({"x": rng.standard_normal((N, 128, TOK), dtype=np.float32).astype(ml_dtypes.bfloat16), "w1": (rng.standard_normal((N, 128, FF * 128), dtype=np.float32) / 8).astype(ml_dtypes.bfloat16), "w2": (rng.standard_normal((N, 128, FF * 128), dtype=np.float32) / 16).astype(ml_dtypes.bfloat16)}, **lists(rng, "uniform"))
def setup_inputs_even(rng):
    d = setup_inputs(rng); d.update(lists(rng, "even"))
    for k in ("x",): d[k] = (d[k].astype(np.float32) * 1024.0).astype(d[k].dtype)
    return d
def setup_inputs_hot(rng):
    d = setup_inputs(rng); d.update(lists(rng, "hot"))
    for k in ("x",): d[k] = (d[k].astype(np.float32) * (1 / 1024.0)).astype(d[k].dtype)
    return d
def setup_inputs_none(rng):
    d = setup_inputs(rng); d.update(lists(rng, "none"))
    return d
def setup_inputs_own(rng):
    d = setup_inputs(rng); d.update(lists(rng, "own"))
    return d
def setup_inputs_skew(rng):
    d = setup_inputs(rng); d.update(lists(rng, "skew"))
    return d
def check_inputs(x):
    bad = []
    if x["ex"].min() < 0 or x["ex"].max() >= N: bad.append("ex out of range")
    E = np.stack([entries(a) for a in x["ex"]])
    if not np.array_equal(np.stack([entries(a) for a in x["pos"]]), np.stack([np.array([np.sum(E[r, :t] == E[r, t]) for t in range(TOK)]) for r in range(N)])): bad.append("pos isn't the place")
    return bad
def reference(x, w1, w2, ex, pos):
    X, W1, W2 = x.astype(np.float64), w1.astype(np.float64), w2.astype(np.float64)
    y = np.zeros((N, 128, TOK))
    for r in range(N):
        E = entries(ex[r]); place = np.array([np.sum(E[:t] == E[t]) for t in range(TOK)])
        for k in range(N):
            m = (E == k) & (place < CAP)
            y[r][:, m] = sum(W2[k][:, 128 * f:128 * f + 128].T @ np.maximum(W1[k][:, 128 * f:128 * f + 128].T @ X[r][:, m], 0.0) for f in range(FF))
    return {"y": y.astype(ml_dtypes.bfloat16)}

@@ -1,0 +1,259 @@
+from concourse.bass import DstId, RemoteDMATransfer
+from concourse.mybir import AluOpType, ActivationFunctionType
+
+N, TOK, CAP = 5, 1024, 256
+WC = 256
+XS = 1024
+YS = 264
+HC = CAP // 2
+
+SCRATCH = {
+    "wb": ("sbuf", [128, N * WC], "bfloat16"),
+    "xs": ("sbuf", [128, TOK], "bfloat16"),
+    "xg": ("sbuf", [128, N * XS], "bfloat16"),
+    "hs": ("sbuf", [128, N * CAP], "bfloat16"),
+    "yg": ("sbuf", [128, N * YS], "bfloat16"),
+    "yo": ("sbuf", [128, TOK], "bfloat16"),
+    "ep": ("sbuf", [16, 128], "int32"),
+    "fa": ("sbuf", [16, 128], "float32"),
+    "fb": ("sbuf", [16, 128], "float32"),
+    "fo": ("sbuf", [16, 128], "float32"),
+    "ones": ("sbuf", [16, 128], "float32"),
+    "rep": ("sbuf", [16, 128], "float32"),
+    "offu": ("sbuf", [128, 128], "uint16"),
+}
+for _l in ("h", "y"):
+    for _h in range(2):
+        for _p in range(2):
+            SCRATCH["p%s%d%d" % (_l, _h, _p)] = ("psum", [128, 512], "float32")
+SEMAPHORES = (["wl", "el", "xl", "sone", "srep", "sz", "sa", "so", "smo", "su", "ssc", "snt", "gv", "gs", "st"]
+              + ["a%d" % k for k in range(N)]
+              + ["%s%d_%d" % (s, h, k) for s in ("m", "r", "n", "c") for h in range(2) for k in range(N)])
+
+
+def _bits(mask):
+    return [b for b in range(16) if (mask >> b) & 1]
+
+
+def _mask(bits):
+    m = 0
+    for b in bits:
+        m |= 1 << b
+    return m
+
+
+def build_plan(cores, topo):
+    n = len(cores)
+    idx = {c: i for i, c in enumerate(cores)}
+
+    def place(c):
+        return (topo.host(c), topo.chip(c))
+
+    direct, local, second = {}, {}, {}
+    entry_load = {c: 0 for c in cores}
+    pass_load = {c: 0 for c in cores}
+    for k, s in enumerate(cores):
+        direct[k], local[k], second[k] = [], [], []
+        groups = {}
+        for d in cores:
+            if d != s:
+                groups.setdefault(place(d), []).append(d)
+        far = []
+        for key, members in groups.items():
+            if key == place(s):
+                local[k] += members
+            elif all(topo.may_write(s, m) for m in members):
+                e = min(members, key=lambda m: (entry_load[m], idx[m]))
+                entry_load[e] += 1
+                direct[k].append(e)
+                second[k] += [(e, m) for m in members if m != e]
+            else:
+                far += members
+        for m in far:
+            via = min([v for v in direct[k] if topo.may_write(v, m)], key=lambda v: (pass_load[v], idx[v]))
+            pass_load[via] += 1
+            second[k].append((via, m))
+
+    def engines(c):
+        out = None
+        for d in cores:
+            if place(d) != place(c) and topo.may_write(c, d):
+                out = topo.mask(c, d) if out is None else out & topo.mask(c, d)
+        inn = 0
+        for d in cores:
+            if d != c and place(d) == place(c):
+                inn = topo.mask(c, d) & ~out
+        return _bits(out), _bits(inn)
+
+    def share(bits, dsts, k):
+        m = 1
+        while m < len(dsts):
+            m *= 2
+        return [(k, d, _mask(bits[i::m])) for i, d in enumerate(dsts)]
+
+    calls = {c: [] for c in cores}
+    arrive, when = {}, {}
+    for k, s in enumerate(cores):
+        off, on = engines(s)
+        crit = [d for d in direct[k] if any(v == d and place(m) != place(v) for v, m in second[k])]
+        rest = [d for d in direct[k] if d not in crit]
+        when[(k, s)] = 0
+        if crit:
+            calls[s].append((None, share(off, crit, k)))
+            for d in crit:
+                when[(k, d)] = 2 if len(crit) == 1 else 3
+        items = share(off, rest, k) + share(on, local[k], k)
+        for d in rest:
+            when[(k, d)] = 4
+        for d in local[k]:
+            when[(k, d)] = 1
+        if items:
+            calls[s].append((None, items))
+    for v in cores:
+        off, on = engines(v)
+        mine = sorted([k for k in range(n) if any(a == v for a, _ in second[k])], key=lambda k: (when[(k, v)], k))
+        for turn, k in enumerate(mine):
+            items = []
+            for a, m in second[k]:
+                if a == v:
+                    far = place(m) != place(v)
+                    items.append((k, m, _mask(off if far else on)))
+                    when[(k, m)] = (10 + turn + when[(k, v)]) if far else (5 + when[(k, v)])
+            calls[v].append((k, items))
+    for c in cores:
+        for _, items in calls[c]:
+            for k, d, mask in items:
+                arrive[(k, d)] = len(_bits(mask))
+    order = {c: sorted(range(n), key=lambda k: (when[(k, c)], k)) for c in cores}
+    return calls, arrive, order
+
+
+def rank_program(g, core, T, topo):
+    r = T.rank_of(core)
+    if r is None:
+        return
+    S = T.sem
+    calls, arrive, order = build_plan(list(T.cores), topo)
+    seq = order[core]
+    v, a, t = g.vector, g.scalar, g.tensor
+
+    def slot(k):
+        return T.wb[:, k * WC:(k + 1) * WC]
+
+    g.sync.dma_start(T.wb[:, r * WC:r * WC + 128], T.w1[:, :]).then_inc(S.wl, 16)
+    a.dma_start(T.wb[:, r * WC + 128:(r + 1) * WC], T.w2[:, :]).then_inc(S.wl, 16)
+    g.sync.dma_start(T.ep[:, 0:64], T.ex[:, :]).then_inc(S.el, 16)
+    a.dma_start(T.ep[:, 64:128], T.pos[:, :]).then_inc(S.el, 16)
+    g.sync.dma_start(T.xs[:, :], T.x[:, :]).then_inc(S.xl, 16)
+
+    v.memset(T.ones[:, :], 1.0).then_inc(S.sone, 1)
+    for k in range(N):
+        v.memset(T.xg[:, k * XS:k * XS + CAP], 0.0).then_inc(S.sz, 1)
+    v.memset(T.yg[:, :], 0.0).then_inc(S.sz, 1)
+
+    g.wait_ge(S.sone, 1)
+    g.affine_select(T.rep[:, :], T.ones[:, :], [[0, 8], [-1, 16]], AluOpType.is_equal, 0.0, 0, 1).then_inc(S.srep, 1)
+
+    sent = 0
+    g.wait_ge(S.wl, 32)
+    for need, items in calls[core]:
+        if need is not None:
+            g.wait_ge(S["a%d" % need], arrive[(need, core)])
+        if len(items) == 1:
+            k, d, mask = items[0]
+            rid, pid = topo.addr(d, core)
+            g.remote_dma(slot(k), slot(k), S["a%d" % k], S.snt, pid, rid, mask)
+        else:
+            trs = []
+            for k, d, mask in items:
+                rid, pid = topo.addr(d, core)
+                trs.append(RemoteDMATransfer(dst_ids=[DstId(rid=rid, pnc=pid)], dma_engine_mask=mask,
+                                             remote_sem=S["a%d" % k], src=slot(k), dst=slot(k)))
+            g.remote_dma_fused(trs, local_sem=S.snt)
+        sent += sum(len(_bits(m)) for _, _, m in items)
+    g.wait_ge(S.snt, sent)
+
+    v.wait_ge(S.el, 32)
+    v.tensor_scalar(T.fa[:, 0:64], T.ep[:, 0:64], float(XS), None, AluOpType.mult).then_inc(S.sa, 1)
+    v.tensor_scalar(T.fa[:, 64:128], T.ep[:, 0:64], float(YS), None, AluOpType.mult).then_inc(S.sa, 1)
+    v.tensor_copy(T.fb[:, 0:64], T.ep[:, 64:128]).then_inc(S.sa, 1)
+    v.tensor_scalar(T.fb[:, 64:128], T.ep[:, 64:128], float(CAP), None, AluOpType.min).then_inc(S.sa, 1)
+    v.wait_ge(S.sa, 4)
+    v.tensor_tensor(T.fo[:, :], T.fa[:, :], T.fb[:, :], AluOpType.add).then_inc(S.so, 1)
+
+    t.wait_ge(S.so, 1)
+    t.wait_ge(S.srep, 1)
+    t.matmul(T.py00[:, 0:128], T.rep[:, :], T.fo[:, :], True, True).then_inc(S.smo, 1)
+
+    v.wait_ge(S.smo, 1)
+    v.tensor_copy(T.offu[:, :], T.py00[:, 0:128]).then_inc(S.su, 1)
+    v.wait_ge(S.su, 1)
+    v.wait_ge(S.xl, 16)
+    v.wait_ge(S.sz, N + 1)
+    v.tensor_copy(T.xg[:, :].indirect(T.offu[:, 0:64]), T.xs[:, :]).then_inc(S.ssc, 1)
+
+    def sem(s, h, k):
+        return S["%s%d_%d" % (s, h, k)]
+
+    def layer1(i):
+        k = seq[i]
+        if k == r:
+            t.wait_ge(S.wl, 32)
+        else:
+            t.wait_ge(S["a%d" % k], arrive[(k, core)])
+        for h in range(2):
+            c = k * XS + h * HC
+            t.matmul(T["ph%d%d" % (h, i % 2)][:, 0:HC], T.wb[:, k * WC:k * WC + 128], T.xg[:, c:c + HC],
+                     True, True).then_inc(sem("m", h, k), 1)
+
+    def layer2(i):
+        k = seq[i]
+        for h in range(2):
+            t.wait_ge(sem("r", h, k), 1)
+            if i >= 2:
+                t.wait_ge(sem("c", h, seq[i - 2]), 1)
+            c = k * CAP + h * HC
+            t.matmul(T["py%d%d" % (h, i % 2)][:, 0:HC], T.wb[:, k * WC + 128:(k + 1) * WC], T.hs[:, c:c + HC],
+                     True, True).then_inc(sem("n", h, k), 1)
+
+    def relu(i):
+        k = seq[i]
+        c = k * CAP
+        a.wait_ge(sem("m", 0, k), 1)
+        a.activation(T.hs[:, c:c + HC], T["ph0%d" % (i % 2)][:, 0:HC], ActivationFunctionType.Relu).then_inc(sem("r", 0, k), 1)
+        v.wait_ge(sem("m", 1, k), 1)
+        v.tensor_scalar(T.hs[:, c + HC:c + CAP], T["ph1%d" % (i % 2)][:, 0:HC], 0.0, None,
+                        AluOpType.max).then_inc(sem("r", 1, k), 1)
+
+    def take(i):
+        k = seq[i]
+        c = k * YS
+        a.wait_ge(sem("n", 0, k), 1)
+        a.activation(T.yg[:, c:c + HC], T["py0%d" % (i % 2)][:, 0:HC], ActivationFunctionType.Copy).then_inc(sem("c", 0, k), 1)
+        v.wait_ge(sem("n", 1, k), 1)
+        v.tensor_copy(T.yg[:, c + HC:c + CAP], T["py1%d" % (i % 2)][:, 0:HC]).then_inc(sem("c", 1, k), 1)
+
+    a.wait_ge(S.sz, N + 1)
+    t.wait_ge(S.ssc, 1)
+    layer1(0)
+    relu(0)
+    for i in range(N):
+        if i + 1 < N:
+            layer1(i + 1)
+            relu(i + 1)
+        layer2(i)
+        take(i)
+
+    H = TOK // 2
+    for k in seq:
+        for h in range(2):
+            v.wait_ge(sem("c", h, k), 1)
+            a.wait_ge(sem("c", h, k), 1)
+    a.wait_ge(S.su, 1)
+    v.tensor_copy(T.yo[:, 0:H], T.yg[:, :].indirect(T.offu[:, 64:96])).then_inc(S.gv, 1)
+    a.activation(T.yo[:, H:TOK], T.yg[:, :].indirect(T.offu[:, 96:128]), ActivationFunctionType.Copy).then_inc(S.gs, 1)
+    g.sync.wait_ge(S.gv, 1)
+    g.sync.dma_start(T.y[:, 0:H], T.yo[:, 0:H]).then_inc(S.st, 16)
+    a.wait_ge(S.gs, 1)
+    a.dma_start(T.y[:, H:TOK], T.yo[:, H:TOK]).then_inc(S.st, 16)
+    g.sync.wait_ge(S.st, 32)

@@ -4,7 +4,7 @@ from concourse.mybir import AluOpType, ActivationFunctionType
 N, TOK, CAP = 5, 1024, 256
 WC = 256
 XS = 1024
-YS = 264
+YS = 257
 HC = CAP // 2
 
 SCRATCH = {
@@ -26,8 +26,10 @@ for _l in ("h", "y"):
     for _h in range(2):
         for _p in range(2):
             SCRATCH["p%s%d%d" % (_l, _h, _p)] = ("psum", [128, 512], "float32")
-SEMAPHORES = (["wl", "el", "xl", "sone", "srep", "sz", "sa", "so", "smo", "su", "ssc", "snt", "gv", "gs", "st"]
+SEMAPHORES = (["wl", "el", "xl", "sone", "srep", "sz", "sa", "so", "smo", "su", "sb", "so2", "smo2", "su2", "ssc", "snt",
+               "gv", "gs", "st"]
               + ["a%d" % k for k in range(N)]
+              + ["b%d" % k for k in range(N)]
               + ["%s%d_%d" % (s, h, k) for s in ("m", "r", "n", "c") for h in range(2) for k in range(N)])
 
 
@@ -92,23 +94,28 @@ def build_plan(cores, topo):
         return [(k, d, _mask(bits[i::m])) for i, d in enumerate(dsts)]
 
     calls = {c: [] for c in cores}
-    arrive, when = {}, {}
+    arrive, when, split = {}, {}, {}
     for k, s in enumerate(cores):
         off, on = engines(s)
         crit = [d for d in direct[k] if any(v == d and place(m) != place(v) for v, m in second[k])]
         rest = [d for d in direct[k] if d not in crit]
         when[(k, s)] = 0
+        split[(k, s)] = False
         if crit:
-            calls[s].append((None, share(off, crit, k)))
+            for layer in range(2):
+                calls[s].append((None, layer, share(off, crit, k)))
             for d in crit:
                 when[(k, d)] = 2 if len(crit) == 1 else 3
+                split[(k, d)] = True
         items = share(off, rest, k) + share(on, local[k], k)
         for d in rest:
             when[(k, d)] = 4
+            split[(k, d)] = False
         for d in local[k]:
             when[(k, d)] = 1
+            split[(k, d)] = False
         if items:
-            calls[s].append((None, items))
+            calls[s].append((None, None, items))
     for v in cores:
         off, on = engines(v)
         mine = sorted([k for k in range(n) if any(a == v for a, _ in second[k])], key=lambda k: (when[(k, v)], k))
@@ -119,13 +126,15 @@ def build_plan(cores, topo):
                     far = place(m) != place(v)
                     items.append((k, m, _mask(off if far else on)))
                     when[(k, m)] = (10 + turn + when[(k, v)]) if far else (5 + when[(k, v)])
-            calls[v].append((k, items))
+                    split[(k, m)] = split[(k, v)]
+            for layer in (range(2) if split[(k, v)] else [None]):
+                calls[v].append((k, layer, items))
     for c in cores:
-        for _, items in calls[c]:
+        for _, _, items in calls[c]:
             for k, d, mask in items:
                 arrive[(k, d)] = len(_bits(mask))
     order = {c: sorted(range(n), key=lambda k: (when[(k, c)], k)) for c in cores}
-    return calls, arrive, order
+    return calls, arrive, split, order
 
 
 def rank_program(g, core, T, topo):
@@ -133,12 +142,17 @@ def rank_program(g, core, T, topo):
     if r is None:
         return
     S = T.sem
-    calls, arrive, order = build_plan(list(T.cores), topo)
+    calls, arrive, split, order = build_plan(list(T.cores), topo)
     seq = order[core]
     v, a, t = g.vector, g.scalar, g.tensor
 
-    def slot(k):
-        return T.wb[:, k * WC:(k + 1) * WC]
+    def piece(k, layer):
+        if layer is None:
+            return T.wb[:, k * WC:(k + 1) * WC]
+        return T.wb[:, k * WC + layer * 128:k * WC + (layer + 1) * 128]
+
+    def landed(k, layer):
+        return S["b%d" % k] if layer == 1 else S["a%d" % k]
 
     g.sync.dma_start(T.wb[:, r * WC:r * WC + 128], T.w1[:, :]).then_inc(S.wl, 16)
     a.dma_start(T.wb[:, r * WC + 128:(r + 1) * WC], T.w2[:, :]).then_inc(S.wl, 16)
@@ -149,48 +163,54 @@ def rank_program(g, core, T, topo):
     v.memset(T.ones[:, :], 1.0).then_inc(S.sone, 1)
     for k in range(N):
         v.memset(T.xg[:, k * XS:k * XS + CAP], 0.0).then_inc(S.sz, 1)
-    v.memset(T.yg[:, :], 0.0).then_inc(S.sz, 1)
+    v.memset(T.yg[:, CAP:N * YS:YS], 0.0).then_inc(S.sz, 1)
 
     g.wait_ge(S.sone, 1)
     g.affine_select(T.rep[:, :], T.ones[:, :], [[0, 8], [-1, 16]], AluOpType.is_equal, 0.0, 0, 1).then_inc(S.srep, 1)
 
     sent = 0
     g.wait_ge(S.wl, 32)
-    for need, items in calls[core]:
+    for need, layer, items in calls[core]:
         if need is not None:
-            g.wait_ge(S["a%d" % need], arrive[(need, core)])
+            g.wait_ge(landed(need, layer), arrive[(need, core)])
         if len(items) == 1:
             k, d, mask = items[0]
             rid, pid = topo.addr(d, core)
-            g.remote_dma(slot(k), slot(k), S["a%d" % k], S.snt, pid, rid, mask)
+            g.remote_dma(piece(k, layer), piece(k, layer), landed(k, layer), S.snt, pid, rid, mask)
         else:
             trs = []
             for k, d, mask in items:
                 rid, pid = topo.addr(d, core)
                 trs.append(RemoteDMATransfer(dst_ids=[DstId(rid=rid, pnc=pid)], dma_engine_mask=mask,
-                                             remote_sem=S["a%d" % k], src=slot(k), dst=slot(k)))
+                                             remote_sem=landed(k, layer), src=piece(k, layer), dst=piece(k, layer)))
             g.remote_dma_fused(trs, local_sem=S.snt)
         sent += sum(len(_bits(m)) for _, _, m in items)
     g.wait_ge(S.snt, sent)
 
     v.wait_ge(S.el, 32)
     v.tensor_scalar(T.fa[:, 0:64], T.ep[:, 0:64], float(XS), None, AluOpType.mult).then_inc(S.sa, 1)
-    v.tensor_scalar(T.fa[:, 64:128], T.ep[:, 0:64], float(YS), None, AluOpType.mult).then_inc(S.sa, 1)
     v.tensor_copy(T.fb[:, 0:64], T.ep[:, 64:128]).then_inc(S.sa, 1)
-    v.tensor_scalar(T.fb[:, 64:128], T.ep[:, 64:128], float(CAP), None, AluOpType.min).then_inc(S.sa, 1)
-    v.wait_ge(S.sa, 4)
-    v.tensor_tensor(T.fo[:, :], T.fa[:, :], T.fb[:, :], AluOpType.add).then_inc(S.so, 1)
+    v.wait_ge(S.sa, 2)
+    v.tensor_tensor(T.fo[:, 0:64], T.fa[:, 0:64], T.fb[:, 0:64], AluOpType.add).then_inc(S.so, 1)
+    v.tensor_scalar(T.fa[:, 64:128], T.ep[:, 0:64], float(YS), None, AluOpType.mult).then_inc(S.sb, 1)
+    v.tensor_scalar(T.fb[:, 64:128], T.ep[:, 64:128], float(CAP), None, AluOpType.min).then_inc(S.sb, 1)
+    v.wait_ge(S.sb, 2)
+    v.tensor_tensor(T.fo[:, 64:128], T.fa[:, 64:128], T.fb[:, 64:128], AluOpType.add).then_inc(S.so2, 1)
 
     t.wait_ge(S.so, 1)
     t.wait_ge(S.srep, 1)
-    t.matmul(T.py00[:, 0:128], T.rep[:, :], T.fo[:, :], True, True).then_inc(S.smo, 1)
+    t.matmul(T.py00[:, 0:64], T.rep[:, :], T.fo[:, 0:64], True, True).then_inc(S.smo, 1)
+    t.wait_ge(S.so2, 1)
+    t.matmul(T.py01[:, 0:64], T.rep[:, :], T.fo[:, 64:128], True, True).then_inc(S.smo2, 1)
 
     v.wait_ge(S.smo, 1)
-    v.tensor_copy(T.offu[:, :], T.py00[:, 0:128]).then_inc(S.su, 1)
+    v.tensor_copy(T.offu[:, 0:64], T.py00[:, 0:64]).then_inc(S.su, 1)
     v.wait_ge(S.su, 1)
     v.wait_ge(S.xl, 16)
     v.wait_ge(S.sz, N + 1)
     v.tensor_copy(T.xg[:, :].indirect(T.offu[:, 0:64]), T.xs[:, :]).then_inc(S.ssc, 1)
+    v.wait_ge(S.smo2, 1)
+    v.tensor_copy(T.offu[:, 64:128], T.py01[:, 0:64]).then_inc(S.su2, 1)
 
     def sem(s, h, k):
         return S["%s%d_%d" % (s, h, k)]
@@ -200,7 +220,7 @@ def rank_program(g, core, T, topo):
         if k == r:
             t.wait_ge(S.wl, 32)
         else:
-            t.wait_ge(S["a%d" % k], arrive[(k, core)])
+            t.wait_ge(landed(k, 0), arrive[(k, core)])
         for h in range(2):
             c = k * XS + h * HC
             t.matmul(T["ph%d%d" % (h, i % 2)][:, 0:HC], T.wb[:, k * WC:k * WC + 128], T.xg[:, c:c + HC],
@@ -208,6 +228,10 @@ def rank_program(g, core, T, topo):
 
     def layer2(i):
         k = seq[i]
+        if i == 1:
+            t.wait_ge(S.su2, 1)
+        if split[(k, core)]:
+            t.wait_ge(landed(k, 1), arrive[(k, core)])
         for h in range(2):
             t.wait_ge(sem("r", h, k), 1)
             if i >= 2:
@@ -249,11 +273,15 @@ def rank_program(g, core, T, topo):
         for h in range(2):
             v.wait_ge(sem("c", h, k), 1)
             a.wait_ge(sem("c", h, k), 1)
-    a.wait_ge(S.su, 1)
+    a.wait_ge(S.su2, 1)
+    v.wait_ge(S.su2, 1)
     v.tensor_copy(T.yo[:, 0:H], T.yg[:, :].indirect(T.offu[:, 64:96])).then_inc(S.gv, 1)
     a.activation(T.yo[:, H:TOK], T.yg[:, :].indirect(T.offu[:, 96:128]), ActivationFunctionType.Copy).then_inc(S.gs, 1)
+    P2 = 64
     g.sync.wait_ge(S.gv, 1)
-    g.sync.dma_start(T.y[:, 0:H], T.yo[:, 0:H]).then_inc(S.st, 16)
+    g.sync.wait_ge(S.gs, 1)
+    g.sync.dma_start(T.y[0:P2, :], T.yo[0:P2, :]).then_inc(S.st, 16)
     a.wait_ge(S.gs, 1)
-    a.dma_start(T.y[:, H:TOK], T.yo[:, H:TOK]).then_inc(S.st, 16)
+    a.wait_ge(S.gv, 1)
+    a.dma_start(T.y[P2:128, :], T.yo[P2:128, :]).then_inc(S.st, 16)
     g.sync.wait_ge(S.st, 32)

@@ -3,34 +3,63 @@ from concourse.mybir import AluOpType, ActivationFunctionType
 
 N, TOK, CAP = 5, 1024, 256
 WC = 256
-XS = 1024
-YS = 257
 HC = CAP // 2
+NS = N * CAP
+LW = NS // 16
+WW = (TOK // 16) * LW
+LQ = TOK // 128
 
 SCRATCH = {
     "wb": ("sbuf", [128, N * WC], "bfloat16"),
     "xs": ("sbuf", [128, TOK], "bfloat16"),
-    "xg": ("sbuf", [128, N * XS], "bfloat16"),
-    "hs": ("sbuf", [128, N * CAP], "bfloat16"),
-    "yg": ("sbuf", [128, N * YS], "bfloat16"),
+    "xg": ("sbuf", [128, NS], "bfloat16"),
+    "hs": ("sbuf", [128, NS], "bfloat16"),
+    "yg": ("sbuf", [128, NS + 8], "bfloat16"),
     "yo": ("sbuf", [128, TOK], "bfloat16"),
+    "exq": ("sbuf", [128, LQ], "int32"),
+    "posq": ("sbuf", [128, LQ], "int32"),
+    "hq": ("sbuf", [128, LQ], "int32"),
+    "q1": ("sbuf", [128, LQ], "float32"),
+    "q2": ("sbuf", [128, LQ], "float32"),
+    "q3": ("sbuf", [128, LQ], "float32"),
+    "q4": ("sbuf", [128, LQ], "float32"),
+    "q5": ("sbuf", [128, LQ], "float32"),
+    "offs": ("sbuf", [128, LQ], "uint16"),
+    "ia": ("sbuf", [128, 128], "int32"),
+    "ib": ("sbuf", [128, 128], "int32"),
+    "i4": ("sbuf", [128, 1], "int32"),
+    "ma": ("sbuf", [128, 1], "float32"),
+    "mb": ("sbuf", [128, 1], "float32"),
+    "va": ("sbuf", [128, 128], "float32"),
+    "vb": ("sbuf", [128, 128], "float32"),
+    "val": ("sbuf", [128, 128], "bfloat16"),
+    "win": ("sbuf", [128, WW], "bfloat16"),
+    "bsl": ("sbuf", [128, 144], "bfloat16"),
+    "offg": ("sbuf", [128, LW], "uint16"),
     "ep": ("sbuf", [16, 128], "int32"),
-    "fa": ("sbuf", [16, 128], "float32"),
-    "fb": ("sbuf", [16, 128], "float32"),
-    "fo": ("sbuf", [16, 128], "float32"),
+    "hy": ("sbuf", [16, 64], "int32"),
+    "f1": ("sbuf", [16, 64], "float32"),
+    "f2": ("sbuf", [16, 64], "float32"),
+    "f3": ("sbuf", [16, 64], "float32"),
+    "f4": ("sbuf", [16, 64], "float32"),
+    "f5": ("sbuf", [16, 64], "float32"),
+    "f6": ("sbuf", [16, 64], "float32"),
+    "f7": ("sbuf", [16, 64], "float32"),
+    "fo": ("sbuf", [16, 64], "float32"),
     "ones": ("sbuf", [16, 128], "float32"),
     "rep": ("sbuf", [16, 128], "float32"),
-    "offu": ("sbuf", [128, 128], "uint16"),
+    "offu": ("sbuf", [128, 64], "uint16"),
 }
 for _l in ("h", "y"):
     for _h in range(2):
         for _p in range(2):
             SCRATCH["p%s%d%d" % (_l, _h, _p)] = ("psum", [128, 512], "float32")
-SEMAPHORES = (["wl", "el", "xl", "sone", "srep", "sz", "sa", "so", "smo", "su", "sb", "so2", "smo2", "su2", "ssc", "snt",
-               "gv", "gs", "st"]
+SEMAPHORES = (["wl", "el", "el2", "xl", "sone", "srep", "sio", "sb0", "sb1", "sz", "s4", "sm", "sv", "sval",
+               "sq1", "sq2", "sq3", "sq4", "ssc", "smo", "su", "sy1", "sy2", "sy3", "sy4", "so2", "smo2", "su2",
+               "snt", "gv", "gs", "st"]
               + ["a%d" % k for k in range(N)]
               + ["b%d" % k for k in range(N)]
-              + ["%s%d_%d" % (s, h, k) for s in ("m", "r", "n", "c") for h in range(2) for k in range(N)])
+              + ["%s%d_%d" % (s, h, k) for s in ("x", "m", "r", "n", "c") for h in range(2) for k in range(N)])
 
 
 def _bits(mask):
@@ -77,62 +106,72 @@ def build_plan(cores, topo):
             second[k].append((via, m))
 
     def engines(c):
-        out = None
+        out, places = None, []
         for d in cores:
             if place(d) != place(c) and topo.may_write(c, d):
                 out = topo.mask(c, d) if out is None else out & topo.mask(c, d)
+                if place(d) not in places:
+                    places.append(place(d))
         inn = 0
         for d in cores:
             if d != c and place(d) == place(c):
                 inn = topo.mask(c, d) & ~out
-        return _bits(out), _bits(inn)
+        m = 1
+        while m < len(places):
+            m *= 2
+        bits = _bits(out)
+        return {p: _mask(bits[i::m]) for i, p in enumerate(places)}, inn
 
-    def share(bits, dsts, k):
+    def share(mask, dsts, k):
+        bits = _bits(mask)
         m = 1
         while m < len(dsts):
             m *= 2
         return [(k, d, _mask(bits[i::m])) for i, d in enumerate(dsts)]
 
-    calls = {c: [] for c in cores}
+    calls = {c: ([], []) for c in cores}
     arrive, when, split = {}, {}, {}
     for k, s in enumerate(cores):
-        off, on = engines(s)
-        crit = [d for d in direct[k] if any(v == d and place(m) != place(v) for v, m in second[k])]
-        rest = [d for d in direct[k] if d not in crit]
+        link, inn = engines(s)
         when[(k, s)] = 0
         split[(k, s)] = False
-        if crit:
-            for layer in range(2):
-                calls[s].append((None, layer, share(off, crit, k)))
-            for d in crit:
-                when[(k, d)] = 2 if len(crit) == 1 else 3
-                split[(k, d)] = True
-        items = share(off, rest, k) + share(on, local[k], k)
-        for d in rest:
-            when[(k, d)] = 4
-            split[(k, d)] = False
+        items = [(k, d, link[place(d)]) for d in direct[k]]
+        for layer in range(2):
+            calls[s][0].append(([], layer, items))
+        for d in direct[k]:
+            when[(k, d)] = 2
+            split[(k, d)] = True
+        if local[k]:
+            calls[s][0].append(([], None, share(inn, local[k], k)))
         for d in local[k]:
             when[(k, d)] = 1
             split[(k, d)] = False
-        if items:
-            calls[s].append((None, None, items))
     for v in cores:
-        off, on = engines(v)
-        mine = sorted([k for k in range(n) if any(a == v for a, _ in second[k])], key=lambda k: (when[(k, v)], k))
-        for turn, k in enumerate(mine):
-            items = []
+        link, inn = engines(v)
+        rounds = []
+        for k in range(n):
             for a, m in second[k]:
-                if a == v:
-                    far = place(m) != place(v)
-                    items.append((k, m, _mask(off if far else on)))
-                    when[(k, m)] = (10 + turn + when[(k, v)]) if far else (5 + when[(k, v)])
-                    split[(k, m)] = split[(k, v)]
-            for layer in (range(2) if split[(k, v)] else [None]):
-                calls[v].append((k, layer, items))
+                if a != v:
+                    continue
+                far = place(m) != place(v)
+                mask = link[place(m)] if far else inn
+                when[(k, m)] = 10 if far else 5
+                split[(k, m)] = True
+                for rd in rounds:
+                    if not any(mask & q for _, _, q in rd):
+                        rd.append((k, m, mask))
+                        break
+                else:
+                    rounds.append([(k, m, mask)])
+        for rd in rounds:
+            need = sorted(set(k for k, _, _ in rd))
+            for layer in range(2):
+                calls[v][1].append((need, layer, rd))
     for c in cores:
-        for _, _, items in calls[c]:
-            for k, d, mask in items:
-                arrive[(k, d)] = len(_bits(mask))
+        for part in calls[c]:
+            for _, _, items in part:
+                for k, d, mask in items:
+                    arrive[(k, d)] = len(_bits(mask))
     order = {c: sorted(range(n), key=lambda k: (when[(k, c)], k)) for c in cores}
     return calls, arrive, split, order
 
@@ -142,6 +181,7 @@ def rank_program(g, core, T, topo):
     if r is None:
         return
     S = T.sem
+    A = AluOpType
     calls, arrive, split, order = build_plan(list(T.cores), topo)
     seq = order[core]
     v, a, t = g.vector, g.scalar, g.tensor
@@ -156,64 +196,111 @@ def rank_program(g, core, T, topo):
 
     g.sync.dma_start(T.wb[:, r * WC:r * WC + 128], T.w1[:, :]).then_inc(S.wl, 16)
     a.dma_start(T.wb[:, r * WC + 128:(r + 1) * WC], T.w2[:, :]).then_inc(S.wl, 16)
+    g.sync.dma_start(T.exq[:, :], T.ex[:, :]).then_inc(S.el2, 16)
+    a.dma_start(T.posq[:, :], T.pos[:, :]).then_inc(S.el2, 16)
     g.sync.dma_start(T.ep[:, 0:64], T.ex[:, :]).then_inc(S.el, 16)
     a.dma_start(T.ep[:, 64:128], T.pos[:, :]).then_inc(S.el, 16)
     g.sync.dma_start(T.xs[:, :], T.x[:, :]).then_inc(S.xl, 16)
 
+    g.iota(T.ib[:, :], [[0, 8], [8, 2], [0, 8]], 0, 1).then_inc(S.sio, 1)
+    g.iota(T.ia[:, :], [[16, 8], [0, 2], [128, 8]], 0, 0).then_inc(S.sio, 1)
+
     v.memset(T.ones[:, :], 1.0).then_inc(S.sone, 1)
-    for k in range(N):
-        v.memset(T.xg[:, k * XS:k * XS + CAP], 0.0).then_inc(S.sz, 1)
-    v.memset(T.yg[:, CAP:N * YS:YS], 0.0).then_inc(S.sz, 1)
+    v.memset(T.bsl[:, :], 0.0).then_inc(S.sb0, 1)
+    v.memset(T.win[:, 0:NS], 0.0).then_inc(S.sz, 1)
+    v.memset(T.yg[:, NS:NS + 8], 0.0).then_inc(S.sz, 1)
+    v.wait_ge(S.sb0, 1)
+    v.memset(T.bsl[:, 0:144:16], 1.0).then_inc(S.sb1, 1)
+    v.wait_ge(S.sio, 2)
+    v.tensor_scalar(T.i4[:, :], T.ib[:, 0:1], 15, None, A.bitwise_and).then_inc(S.s4, 1)
+    v.wait_ge(S.s4, 1)
+    v.tensor_scalar(T.mb[:, :], T.i4[:, :], 0.0, 0.125, A.is_equal, A.mult).then_inc(S.sm, 1)
+    v.tensor_scalar(T.ma[:, :], T.i4[:, :], 8.0, None, A.is_equal).then_inc(S.sm, 1)
+    v.wait_ge(S.sm, 2)
+    v.tensor_scalar(T.va[:, :], T.ia[:, :], T.ma[:, 0:1], None, A.mult).then_inc(S.sv, 1)
+    v.tensor_scalar(T.vb[:, :], T.ib[:, :], T.mb[:, 0:1], None, A.mult).then_inc(S.sv, 1)
+    v.wait_ge(S.sv, 2)
+    v.tensor_tensor(T.val[:, :], T.va[:, :], T.vb[:, :], A.add).then_inc(S.sval, 1)
 
-    g.wait_ge(S.sone, 1)
-    g.affine_select(T.rep[:, :], T.ones[:, :], [[0, 8], [-1, 16]], AluOpType.is_equal, 0.0, 0, 1).then_inc(S.srep, 1)
+    sent = [0]
 
-    sent = 0
-    g.wait_ge(S.wl, 32)
-    for need, layer, items in calls[core]:
-        if need is not None:
-            g.wait_ge(landed(need, layer), arrive[(need, core)])
-        if len(items) == 1:
-            k, d, mask = items[0]
-            rid, pid = topo.addr(d, core)
-            g.remote_dma(piece(k, layer), piece(k, layer), landed(k, layer), S.snt, pid, rid, mask)
-        else:
-            trs = []
-            for k, d, mask in items:
+    def issue(part):
+        for need, layer, items in part:
+            for k in need:
+                g.wait_ge(landed(k, layer), arrive[(k, core)])
+            if len(items) == 1:
+                k, d, mask = items[0]
                 rid, pid = topo.addr(d, core)
-                trs.append(RemoteDMATransfer(dst_ids=[DstId(rid=rid, pnc=pid)], dma_engine_mask=mask,
-                                             remote_sem=landed(k, layer), src=piece(k, layer), dst=piece(k, layer)))
-            g.remote_dma_fused(trs, local_sem=S.snt)
-        sent += sum(len(_bits(m)) for _, _, m in items)
-    g.wait_ge(S.snt, sent)
+                g.remote_dma(piece(k, layer), piece(k, layer), landed(k, layer), S.snt, pid, rid, mask)
+            else:
+                trs = []
+                for k, d, mask in items:
+                    rid, pid = topo.addr(d, core)
+                    trs.append(RemoteDMATransfer(dst_ids=[DstId(rid=rid, pnc=pid)], dma_engine_mask=mask,
+                                                 remote_sem=landed(k, layer), src=piece(k, layer), dst=piece(k, layer)))
+                g.remote_dma_fused(trs, local_sem=S.snt)
+            sent[0] += sum(len(_bits(m)) for _, _, m in items)
 
+    g.wait_ge(S.wl, 32)
+    issue(calls[core][0])
+    g.wait_ge(S.sone, 1)
+    g.affine_select(T.rep[:, :], T.ones[:, :], [[0, 8], [-1, 16]], A.is_equal, 0.0, 0, 1).then_inc(S.srep, 1)
+    issue(calls[core][1])
+    g.wait_ge(S.snt, sent[0])
+
+    v.wait_ge(S.el2, 32)
+    v.tensor_scalar(T.hq[:, :], T.posq[:, :], 4, None, A.logical_shift_right).then_inc(S.sq1, 1)
+    v.tensor_scalar(T.q1[:, :], T.exq[:, :], 16.0, None, A.mult).then_inc(S.sq1, 1)
+    v.tensor_copy(T.q2[:, :], T.posq[:, :]).then_inc(S.sq1, 1)
+    v.wait_ge(S.sq1, 3)
+    v.tensor_scalar(T.q3[:, :], T.hq[:, :], float(LW - 16), None, A.mult).then_inc(S.sq2, 1)
+    v.tensor_tensor(T.q4[:, :], T.q1[:, :], T.q2[:, :], A.add).then_inc(S.sq2, 1)
+    v.wait_ge(S.sq2, 2)
+    v.tensor_tensor(T.q5[:, :], T.q3[:, :], T.q4[:, :], A.add).then_inc(S.sq3, 1)
+    v.wait_ge(S.sq3, 1)
+    v.tensor_copy(T.offs[:, :], T.q5[:, :]).then_inc(S.sq4, 1)
+    v.wait_ge(S.sq4, 1)
+    v.wait_ge(S.sval, 1)
+    v.wait_ge(S.sz, 2)
+    v.tensor_copy(T.win[:, :].indirect(T.offs[:, :]), T.val[:, :]).then_inc(S.ssc, 1)
+
+    t.wait_ge(S.ssc, 1)
+    t.wait_ge(S.sb1, 1)
+    for q in range(16):
+        mm = t.matmul(T.py00[:, 0:LW], T.bsl[:, 16 - q:144 - q], T.win[:, q * LW:(q + 1) * LW], q == 0, q == 15)
+    mm.then_inc(S.smo, 1)
+
+    ex16, pos16 = T.ep[:, 0:64], T.ep[:, 64:128]
     v.wait_ge(S.el, 32)
-    v.tensor_scalar(T.fa[:, 0:64], T.ep[:, 0:64], float(XS), None, AluOpType.mult).then_inc(S.sa, 1)
-    v.tensor_copy(T.fb[:, 0:64], T.ep[:, 64:128]).then_inc(S.sa, 1)
-    v.wait_ge(S.sa, 2)
-    v.tensor_tensor(T.fo[:, 0:64], T.fa[:, 0:64], T.fb[:, 0:64], AluOpType.add).then_inc(S.so, 1)
-    v.tensor_scalar(T.fa[:, 64:128], T.ep[:, 0:64], float(YS), None, AluOpType.mult).then_inc(S.sb, 1)
-    v.tensor_scalar(T.fb[:, 64:128], T.ep[:, 64:128], float(CAP), None, AluOpType.min).then_inc(S.sb, 1)
-    v.wait_ge(S.sb, 2)
-    v.tensor_tensor(T.fo[:, 64:128], T.fa[:, 64:128], T.fb[:, 64:128], AluOpType.add).then_inc(S.so2, 1)
-
-    t.wait_ge(S.so, 1)
-    t.wait_ge(S.srep, 1)
-    t.matmul(T.py00[:, 0:64], T.rep[:, :], T.fo[:, 0:64], True, True).then_inc(S.smo, 1)
-    t.wait_ge(S.so2, 1)
-    t.matmul(T.py01[:, 0:64], T.rep[:, :], T.fo[:, 64:128], True, True).then_inc(S.smo2, 1)
+    v.tensor_scalar(T.hy[:, :], pos16, 4, None, A.logical_shift_right).then_inc(S.sy1, 1)
+    v.tensor_scalar(T.f1[:, :], ex16, float(CAP), None, A.mult).then_inc(S.sy1, 1)
+    v.tensor_scalar(T.f2[:, :], pos16, 16.0, None, A.mult).then_inc(S.sy1, 1)
+    v.tensor_scalar(T.f3[:, :], pos16, float(CAP), 8192.0, A.is_ge, A.mult).then_inc(S.sy1, 1)
+    v.wait_ge(S.sy1, 4)
+    v.tensor_scalar(T.f4[:, :], T.hy[:, :], -255.0, None, A.mult).then_inc(S.sy2, 1)
+    v.tensor_tensor(T.f5[:, :], T.f1[:, :], T.f2[:, :], A.add).then_inc(S.sy2, 1)
+    v.wait_ge(S.sy2, 2)
+    v.tensor_tensor(T.f6[:, :], T.f3[:, :], T.f4[:, :], A.add).then_inc(S.sy3, 1)
+    v.wait_ge(S.sy3, 1)
+    v.tensor_tensor(T.f7[:, :], T.f5[:, :], T.f6[:, :], A.add).then_inc(S.sy4, 1)
+    v.wait_ge(S.sy4, 1)
+    v.tensor_scalar(T.fo[:, :], T.f7[:, :], float(NS), None, A.min).then_inc(S.so2, 1)
 
     v.wait_ge(S.smo, 1)
-    v.tensor_copy(T.offu[:, 0:64], T.py00[:, 0:64]).then_inc(S.su, 1)
-    v.wait_ge(S.su, 1)
-    v.wait_ge(S.xl, 16)
-    v.wait_ge(S.sz, N + 1)
-    v.tensor_copy(T.xg[:, :].indirect(T.offu[:, 0:64]), T.xs[:, :]).then_inc(S.ssc, 1)
-    v.wait_ge(S.smo2, 1)
-    v.tensor_copy(T.offu[:, 64:128], T.py01[:, 0:64]).then_inc(S.su2, 1)
+    v.tensor_copy(T.offg[:, :], T.py00[:, 0:LW]).then_inc(S.su, 1)
 
     def sem(s, h, k):
         return S["%s%d_%d" % (s, h, k)]
+
+    v.wait_ge(S.su, 1)
+    v.wait_ge(S.xl, 16)
+    a.wait_ge(S.su, 1)
+    a.wait_ge(S.xl, 16)
+    for k in seq:
+        c, o = k * CAP, k * 16
+        a.activation(T.xg[:, c:c + HC], T.xs[:, :].indirect(T.offg[:, o:o + 8]),
+                     ActivationFunctionType.Copy).then_inc(sem("x", 0, k), 1)
+        v.tensor_copy(T.xg[:, c + HC:c + CAP], T.xs[:, :].indirect(T.offg[:, o + 8:o + 16])).then_inc(sem("x", 1, k), 1)
 
     def layer1(i):
         k = seq[i]
@@ -222,12 +309,15 @@ def rank_program(g, core, T, topo):
         else:
             t.wait_ge(landed(k, 0), arrive[(k, core)])
         for h in range(2):
-            c = k * XS + h * HC
+            c = k * CAP + h * HC
+            t.wait_ge(sem("x", h, k), 1)
             t.matmul(T["ph%d%d" % (h, i % 2)][:, 0:HC], T.wb[:, k * WC:k * WC + 128], T.xg[:, c:c + HC],
                      True, True).then_inc(sem("m", h, k), 1)
 
     def layer2(i):
         k = seq[i]
+        if i == 0:
+            t.wait_ge(S.su, 1)
         if i == 1:
             t.wait_ge(S.su2, 1)
         if split[(k, core)]:
@@ -247,18 +337,17 @@ def rank_program(g, core, T, topo):
         a.activation(T.hs[:, c:c + HC], T["ph0%d" % (i % 2)][:, 0:HC], ActivationFunctionType.Relu).then_inc(sem("r", 0, k), 1)
         v.wait_ge(sem("m", 1, k), 1)
         v.tensor_scalar(T.hs[:, c + HC:c + CAP], T["ph1%d" % (i % 2)][:, 0:HC], 0.0, None,
-                        AluOpType.max).then_inc(sem("r", 1, k), 1)
+                        A.max).then_inc(sem("r", 1, k), 1)
 
     def take(i):
         k = seq[i]
-        c = k * YS
+        c = k * CAP
         a.wait_ge(sem("n", 0, k), 1)
         a.activation(T.yg[:, c:c + HC], T["py0%d" % (i % 2)][:, 0:HC], ActivationFunctionType.Copy).then_inc(sem("c", 0, k), 1)
         v.wait_ge(sem("n", 1, k), 1)
         v.tensor_copy(T.yg[:, c + HC:c + CAP], T["py1%d" % (i % 2)][:, 0:HC]).then_inc(sem("c", 1, k), 1)
 
-    a.wait_ge(S.sz, N + 1)
-    t.wait_ge(S.ssc, 1)
+    a.wait_ge(S.sz, 2)
     layer1(0)
     relu(0)
     for i in range(N):
@@ -267,6 +356,12 @@ def rank_program(g, core, T, topo):
             relu(i + 1)
         layer2(i)
         take(i)
+        if i == 0:
+            t.wait_ge(S.so2, 1)
+            t.wait_ge(S.srep, 1)
+            t.matmul(T.py01[:, 0:64], T.rep[:, :], T.fo[:, :], True, True).then_inc(S.smo2, 1)
+            v.wait_ge(S.smo2, 1)
+            v.tensor_copy(T.offu[:, :], T.py01[:, 0:64]).then_inc(S.su2, 1)
 
     H = TOK // 2
     for k in seq:
@@ -275,8 +370,8 @@ def rank_program(g, core, T, topo):
             a.wait_ge(sem("c", h, k), 1)
     a.wait_ge(S.su2, 1)
     v.wait_ge(S.su2, 1)
-    v.tensor_copy(T.yo[:, 0:H], T.yg[:, :].indirect(T.offu[:, 64:96])).then_inc(S.gv, 1)
-    a.activation(T.yo[:, H:TOK], T.yg[:, :].indirect(T.offu[:, 96:128]), ActivationFunctionType.Copy).then_inc(S.gs, 1)
+    v.tensor_copy(T.yo[:, 0:H], T.yg[:, :].indirect(T.offu[:, 0:32])).then_inc(S.gv, 1)
+    a.activation(T.yo[:, H:TOK], T.yg[:, :].indirect(T.offu[:, 32:64]), ActivationFunctionType.Copy).then_inc(S.gs, 1)
     P2 = 64
     g.sync.wait_ge(S.gv, 1)
     g.sync.wait_ge(S.gs, 1)

from concourse.bass import DstId, RemoteDMATransfer
from concourse.mybir import AluOpType, ActivationFunctionType

N, TOK, CAP = 5, 1024, 256
WC = 256
HC = CAP // 2
NS = N * CAP
LW = NS // 16
WW = (TOK // 16) * LW
LQ = TOK // 128

SCRATCH = {
    "wb": ("sbuf", [128, N * WC], "bfloat16"),
    "xs": ("sbuf", [128, TOK], "bfloat16"),
    "xg": ("sbuf", [128, NS], "bfloat16"),
    "hs": ("sbuf", [128, NS], "bfloat16"),
    "yg": ("sbuf", [128, NS + 8], "bfloat16"),
    "yo": ("sbuf", [128, TOK], "bfloat16"),
    "exq": ("sbuf", [128, LQ], "int32"),
    "posq": ("sbuf", [128, LQ], "int32"),
    "hq": ("sbuf", [128, LQ], "int32"),
    "q1": ("sbuf", [128, LQ], "float32"),
    "q2": ("sbuf", [128, LQ], "float32"),
    "q3": ("sbuf", [128, LQ], "float32"),
    "q4": ("sbuf", [128, LQ], "float32"),
    "q5": ("sbuf", [128, LQ], "float32"),
    "offs": ("sbuf", [128, LQ], "uint16"),
    "ia": ("sbuf", [128, 128], "int32"),
    "ib": ("sbuf", [128, 128], "int32"),
    "i4": ("sbuf", [128, 1], "int32"),
    "ma": ("sbuf", [128, 1], "float32"),
    "mb": ("sbuf", [128, 1], "float32"),
    "va": ("sbuf", [128, 128], "float32"),
    "vb": ("sbuf", [128, 128], "float32"),
    "val": ("sbuf", [128, 128], "bfloat16"),
    "win": ("sbuf", [128, WW], "bfloat16"),
    "bsl": ("sbuf", [128, 144], "bfloat16"),
    "offg": ("sbuf", [128, LW], "uint16"),
    "ep": ("sbuf", [16, 128], "int32"),
    "hy": ("sbuf", [16, 64], "int32"),
    "f1": ("sbuf", [16, 64], "float32"),
    "f2": ("sbuf", [16, 64], "float32"),
    "f3": ("sbuf", [16, 64], "float32"),
    "f4": ("sbuf", [16, 64], "float32"),
    "f5": ("sbuf", [16, 64], "float32"),
    "f6": ("sbuf", [16, 64], "float32"),
    "f7": ("sbuf", [16, 64], "float32"),
    "fo": ("sbuf", [16, 64], "float32"),
    "ones": ("sbuf", [16, 128], "float32"),
    "rep": ("sbuf", [16, 128], "float32"),
    "offu": ("sbuf", [128, 64], "uint16"),
}
for _l in ("h", "y"):
    for _h in range(2):
        for _p in range(2):
            SCRATCH["p%s%d%d" % (_l, _h, _p)] = ("psum", [128, 512], "float32")
SEMAPHORES = (["wl", "el", "el2", "xl", "sone", "srep", "sio", "sb0", "sb1", "sz", "s4", "sm", "sv", "sval",
               "sq1", "sq2", "sq3", "sq4", "ssc", "smo", "su", "sy1", "sy2", "sy3", "sy4", "so2", "smo2", "su2",
               "snt", "gv", "gs", "st"]
              + ["a%d" % k for k in range(N)]
              + ["b%d" % k for k in range(N)]
              + ["%s%d_%d" % (s, h, k) for s in ("x", "m", "r", "n", "c") for h in range(2) for k in range(N)])


def _bits(mask):
    return [b for b in range(16) if (mask >> b) & 1]


def _mask(bits):
    m = 0
    for b in bits:
        m |= 1 << b
    return m


def build_plan(cores, topo):
    n = len(cores)
    idx = {c: i for i, c in enumerate(cores)}

    def place(c):
        return (topo.host(c), topo.chip(c))

    direct, local, second = {}, {}, {}
    entry_load = {c: 0 for c in cores}
    pass_load = {c: 0 for c in cores}
    for k, s in enumerate(cores):
        direct[k], local[k], second[k] = [], [], []
        groups = {}
        for d in cores:
            if d != s:
                groups.setdefault(place(d), []).append(d)
        far = []
        for key, members in groups.items():
            if key == place(s):
                local[k] += members
            elif all(topo.may_write(s, m) for m in members):
                e = min(members, key=lambda m: (entry_load[m], idx[m]))
                entry_load[e] += 1
                direct[k].append(e)
                second[k] += [(e, m) for m in members if m != e]
            else:
                far += members
        for m in far:
            via = min([v for v in direct[k] if topo.may_write(v, m)], key=lambda v: (pass_load[v], idx[v]))
            pass_load[via] += 1
            second[k].append((via, m))

    def engines(c):
        out, places = None, []
        for d in cores:
            if place(d) != place(c) and topo.may_write(c, d):
                out = topo.mask(c, d) if out is None else out & topo.mask(c, d)
                if place(d) not in places:
                    places.append(place(d))
        inn = 0
        for d in cores:
            if d != c and place(d) == place(c):
                inn = topo.mask(c, d) & ~out
        m = 1
        while m < len(places):
            m *= 2
        bits = _bits(out)
        return {p: _mask(bits[i::m]) for i, p in enumerate(places)}, inn

    def share(mask, dsts, k):
        bits = _bits(mask)
        m = 1
        while m < len(dsts):
            m *= 2
        return [(k, d, _mask(bits[i::m])) for i, d in enumerate(dsts)]

    calls = {c: ([], []) for c in cores}
    arrive, when, split = {}, {}, {}
    for k, s in enumerate(cores):
        link, inn = engines(s)
        when[(k, s)] = 0
        split[(k, s)] = False
        items = [(k, d, link[place(d)]) for d in direct[k]]
        for layer in range(2):
            calls[s][0].append(([], layer, items))
        for d in direct[k]:
            when[(k, d)] = 2
            split[(k, d)] = True
        if local[k]:
            calls[s][0].append(([], None, share(inn, local[k], k)))
        for d in local[k]:
            when[(k, d)] = 1
            split[(k, d)] = False
    for v in cores:
        link, inn = engines(v)
        rounds = []
        for k in range(n):
            for a, m in second[k]:
                if a != v:
                    continue
                far = place(m) != place(v)
                mask = link[place(m)] if far else inn
                when[(k, m)] = 10 if far else 5
                split[(k, m)] = True
                for rd in rounds:
                    if not any(mask & q for _, _, q in rd):
                        rd.append((k, m, mask))
                        break
                else:
                    rounds.append([(k, m, mask)])
        for rd in rounds:
            need = sorted(set(k for k, _, _ in rd))
            for layer in range(2):
                calls[v][1].append((need, layer, rd))
    for c in cores:
        for part in calls[c]:
            for _, _, items in part:
                for k, d, mask in items:
                    arrive[(k, d)] = len(_bits(mask))
    order = {c: sorted(range(n), key=lambda k: (when[(k, c)], k)) for c in cores}
    return calls, arrive, split, order


def rank_program(g, core, T, topo):
    r = T.rank_of(core)
    if r is None:
        return
    S = T.sem
    A = AluOpType
    calls, arrive, split, order = build_plan(list(T.cores), topo)
    seq = order[core]
    v, a, t = g.vector, g.scalar, g.tensor

    def piece(k, layer):
        if layer is None:
            return T.wb[:, k * WC:(k + 1) * WC]
        return T.wb[:, k * WC + layer * 128:k * WC + (layer + 1) * 128]

    def landed(k, layer):
        return S["b%d" % k] if layer == 1 else S["a%d" % k]

    g.sync.dma_start(T.wb[:, r * WC:r * WC + 128], T.w1[:, :]).then_inc(S.wl, 16)
    a.dma_start(T.wb[:, r * WC + 128:(r + 1) * WC], T.w2[:, :]).then_inc(S.wl, 16)
    g.sync.dma_start(T.exq[:, :], T.ex[:, :]).then_inc(S.el2, 16)
    a.dma_start(T.posq[:, :], T.pos[:, :]).then_inc(S.el2, 16)
    g.sync.dma_start(T.ep[:, 0:64], T.ex[:, :]).then_inc(S.el, 16)
    a.dma_start(T.ep[:, 64:128], T.pos[:, :]).then_inc(S.el, 16)
    g.sync.dma_start(T.xs[:, :], T.x[:, :]).then_inc(S.xl, 16)

    g.iota(T.ib[:, :], [[0, 8], [8, 2], [0, 8]], 0, 1).then_inc(S.sio, 1)
    g.iota(T.ia[:, :], [[16, 8], [0, 2], [128, 8]], 0, 0).then_inc(S.sio, 1)

    v.memset(T.ones[:, :], 1.0).then_inc(S.sone, 1)
    v.memset(T.bsl[:, :], 0.0).then_inc(S.sb0, 1)
    v.memset(T.win[:, 0:NS], 0.0).then_inc(S.sz, 1)
    v.memset(T.yg[:, NS:NS + 8], 0.0).then_inc(S.sz, 1)
    v.wait_ge(S.sb0, 1)
    v.memset(T.bsl[:, 0:144:16], 1.0).then_inc(S.sb1, 1)
    v.wait_ge(S.sio, 2)
    v.tensor_scalar(T.i4[:, :], T.ib[:, 0:1], 15, None, A.bitwise_and).then_inc(S.s4, 1)
    v.wait_ge(S.s4, 1)
    v.tensor_scalar(T.mb[:, :], T.i4[:, :], 0.0, 0.125, A.is_equal, A.mult).then_inc(S.sm, 1)
    v.tensor_scalar(T.ma[:, :], T.i4[:, :], 8.0, None, A.is_equal).then_inc(S.sm, 1)
    v.wait_ge(S.sm, 2)
    v.tensor_scalar(T.va[:, :], T.ia[:, :], T.ma[:, 0:1], None, A.mult).then_inc(S.sv, 1)
    v.tensor_scalar(T.vb[:, :], T.ib[:, :], T.mb[:, 0:1], None, A.mult).then_inc(S.sv, 1)
    v.wait_ge(S.sv, 2)
    v.tensor_tensor(T.val[:, :], T.va[:, :], T.vb[:, :], A.add).then_inc(S.sval, 1)

    sent = [0]

    def issue(part):
        for need, layer, items in part:
            for k in need:
                g.wait_ge(landed(k, layer), arrive[(k, core)])
            if len(items) == 1:
                k, d, mask = items[0]
                rid, pid = topo.addr(d, core)
                g.remote_dma(piece(k, layer), piece(k, layer), landed(k, layer), S.snt, pid, rid, mask)
            else:
                trs = []
                for k, d, mask in items:
                    rid, pid = topo.addr(d, core)
                    trs.append(RemoteDMATransfer(dst_ids=[DstId(rid=rid, pnc=pid)], dma_engine_mask=mask,
                                                 remote_sem=landed(k, layer), src=piece(k, layer), dst=piece(k, layer)))
                g.remote_dma_fused(trs, local_sem=S.snt)
            sent[0] += sum(len(_bits(m)) for _, _, m in items)

    g.wait_ge(S.wl, 32)
    issue(calls[core][0])
    g.wait_ge(S.sone, 1)
    g.affine_select(T.rep[:, :], T.ones[:, :], [[0, 8], [-1, 16]], A.is_equal, 0.0, 0, 1).then_inc(S.srep, 1)
    issue(calls[core][1])
    g.wait_ge(S.snt, sent[0])

    v.wait_ge(S.el2, 32)
    v.tensor_scalar(T.hq[:, :], T.posq[:, :], 4, None, A.logical_shift_right).then_inc(S.sq1, 1)
    v.tensor_scalar(T.q1[:, :], T.exq[:, :], 16.0, None, A.mult).then_inc(S.sq1, 1)
    v.tensor_copy(T.q2[:, :], T.posq[:, :]).then_inc(S.sq1, 1)
    v.wait_ge(S.sq1, 3)
    v.tensor_scalar(T.q3[:, :], T.hq[:, :], float(LW - 16), None, A.mult).then_inc(S.sq2, 1)
    v.tensor_tensor(T.q4[:, :], T.q1[:, :], T.q2[:, :], A.add).then_inc(S.sq2, 1)
    v.wait_ge(S.sq2, 2)
    v.tensor_tensor(T.q5[:, :], T.q3[:, :], T.q4[:, :], A.add).then_inc(S.sq3, 1)
    v.wait_ge(S.sq3, 1)
    v.tensor_copy(T.offs[:, :], T.q5[:, :]).then_inc(S.sq4, 1)
    v.wait_ge(S.sq4, 1)
    v.wait_ge(S.sval, 1)
    v.wait_ge(S.sz, 2)
    v.tensor_copy(T.win[:, :].indirect(T.offs[:, :]), T.val[:, :]).then_inc(S.ssc, 1)

    t.wait_ge(S.ssc, 1)
    t.wait_ge(S.sb1, 1)
    for q in range(16):
        mm = t.matmul(T.py00[:, 0:LW], T.bsl[:, 16 - q:144 - q], T.win[:, q * LW:(q + 1) * LW], q == 0, q == 15)
    mm.then_inc(S.smo, 1)

    ex16, pos16 = T.ep[:, 0:64], T.ep[:, 64:128]
    v.wait_ge(S.el, 32)
    v.tensor_scalar(T.hy[:, :], pos16, 4, None, A.logical_shift_right).then_inc(S.sy1, 1)
    v.tensor_scalar(T.f1[:, :], ex16, float(CAP), None, A.mult).then_inc(S.sy1, 1)
    v.tensor_scalar(T.f2[:, :], pos16, 16.0, None, A.mult).then_inc(S.sy1, 1)
    v.tensor_scalar(T.f3[:, :], pos16, float(CAP), 8192.0, A.is_ge, A.mult).then_inc(S.sy1, 1)
    v.wait_ge(S.sy1, 4)
    v.tensor_scalar(T.f4[:, :], T.hy[:, :], -255.0, None, A.mult).then_inc(S.sy2, 1)
    v.tensor_tensor(T.f5[:, :], T.f1[:, :], T.f2[:, :], A.add).then_inc(S.sy2, 1)
    v.wait_ge(S.sy2, 2)
    v.tensor_tensor(T.f6[:, :], T.f3[:, :], T.f4[:, :], A.add).then_inc(S.sy3, 1)
    v.wait_ge(S.sy3, 1)
    v.tensor_tensor(T.f7[:, :], T.f5[:, :], T.f6[:, :], A.add).then_inc(S.sy4, 1)
    v.wait_ge(S.sy4, 1)
    v.tensor_scalar(T.fo[:, :], T.f7[:, :], float(NS), None, A.min).then_inc(S.so2, 1)

    v.wait_ge(S.smo, 1)
    v.tensor_copy(T.offg[:, :], T.py00[:, 0:LW]).then_inc(S.su, 1)

    def sem(s, h, k):
        return S["%s%d_%d" % (s, h, k)]

    v.wait_ge(S.su, 1)
    v.wait_ge(S.xl, 16)
    a.wait_ge(S.su, 1)
    a.wait_ge(S.xl, 16)
    for k in seq:
        c, o = k * CAP, k * 16
        a.activation(T.xg[:, c:c + HC], T.xs[:, :].indirect(T.offg[:, o:o + 8]),
                     ActivationFunctionType.Copy).then_inc(sem("x", 0, k), 1)
        v.tensor_copy(T.xg[:, c + HC:c + CAP], T.xs[:, :].indirect(T.offg[:, o + 8:o + 16])).then_inc(sem("x", 1, k), 1)

    def layer1(i):
        k = seq[i]
        if k == r:
            t.wait_ge(S.wl, 32)
        else:
            t.wait_ge(landed(k, 0), arrive[(k, core)])
        for h in range(2):
            c = k * CAP + h * HC
            t.wait_ge(sem("x", h, k), 1)
            t.matmul(T["ph%d%d" % (h, i % 2)][:, 0:HC], T.wb[:, k * WC:k * WC + 128], T.xg[:, c:c + HC],
                     True, True).then_inc(sem("m", h, k), 1)

    def layer2(i):
        k = seq[i]
        if i == 0:
            t.wait_ge(S.su, 1)
        if i == 1:
            t.wait_ge(S.su2, 1)
        if split[(k, core)]:
            t.wait_ge(landed(k, 1), arrive[(k, core)])
        for h in range(2):
            t.wait_ge(sem("r", h, k), 1)
            if i >= 2:
                t.wait_ge(sem("c", h, seq[i - 2]), 1)
            c = k * CAP + h * HC
            t.matmul(T["py%d%d" % (h, i % 2)][:, 0:HC], T.wb[:, k * WC + 128:(k + 1) * WC], T.hs[:, c:c + HC],
                     True, True).then_inc(sem("n", h, k), 1)

    def relu(i):
        k = seq[i]
        c = k * CAP
        a.wait_ge(sem("m", 0, k), 1)
        a.activation(T.hs[:, c:c + HC], T["ph0%d" % (i % 2)][:, 0:HC], ActivationFunctionType.Relu).then_inc(sem("r", 0, k), 1)
        v.wait_ge(sem("m", 1, k), 1)
        v.tensor_scalar(T.hs[:, c + HC:c + CAP], T["ph1%d" % (i % 2)][:, 0:HC], 0.0, None,
                        A.max).then_inc(sem("r", 1, k), 1)

    def take(i):
        k = seq[i]
        c = k * CAP
        a.wait_ge(sem("n", 0, k), 1)
        a.activation(T.yg[:, c:c + HC], T["py0%d" % (i % 2)][:, 0:HC], ActivationFunctionType.Copy).then_inc(sem("c", 0, k), 1)
        v.wait_ge(sem("n", 1, k), 1)
        v.tensor_copy(T.yg[:, c + HC:c + CAP], T["py1%d" % (i % 2)][:, 0:HC]).then_inc(sem("c", 1, k), 1)

    a.wait_ge(S.sz, 2)
    layer1(0)
    relu(0)
    for i in range(N):
        if i + 1 < N:
            layer1(i + 1)
            relu(i + 1)
        layer2(i)
        take(i)
        if i == 0:
            t.wait_ge(S.so2, 1)
            t.wait_ge(S.srep, 1)
            t.matmul(T.py01[:, 0:64], T.rep[:, :], T.fo[:, :], True, True).then_inc(S.smo2, 1)
            v.wait_ge(S.smo2, 1)
            v.tensor_copy(T.offu[:, :], T.py01[:, 0:64]).then_inc(S.su2, 1)

    H = TOK // 2
    for k in seq:
        for h in range(2):
            v.wait_ge(sem("c", h, k), 1)
            a.wait_ge(sem("c", h, k), 1)
    a.wait_ge(S.su2, 1)
    v.wait_ge(S.su2, 1)
    v.tensor_copy(T.yo[:, 0:H], T.yg[:, :].indirect(T.offu[:, 0:32])).then_inc(S.gv, 1)
    a.activation(T.yo[:, H:TOK], T.yg[:, :].indirect(T.offu[:, 32:64]), ActivationFunctionType.Copy).then_inc(S.gs, 1)
    P2 = 64
    g.sync.wait_ge(S.gv, 1)
    g.sync.wait_ge(S.gs, 1)
    g.sync.dma_start(T.y[0:P2, :], T.yo[0:P2, :]).then_inc(S.st, 16)
    a.wait_ge(S.gs, 1)
    a.wait_ge(S.gv, 1)
    a.dma_start(T.y[P2:128, :], T.yo[P2:128, :]).then_inc(S.st, 16)
    g.sync.wait_ge(S.st, 32)
